import numpy as np
import ml_dtypes


def mxq(x, axis, fmt="e4m3"):
    dtype, down = {"e4m3": (ml_dtypes.float8_e4m3fn, 7), "e5m2": (ml_dtypes.float8_e5m2, 14)}[fmt]
    v = np.moveaxis(np.asarray(x, np.float32).astype(ml_dtypes.bfloat16).astype(np.float64), axis, -1)
    blocks = v.reshape(v.shape[:-1] + (-1, 32))
    amax = np.abs(blocks).max(-1, keepdims=True)
    byte = np.maximum(np.where(amax > 0, np.frexp(amax)[1] - 1 + 127, 0) - down, 1)
    scale = np.exp2(byte - 127.0)
    codes = (blocks / scale).astype(np.float32).astype(dtype).astype(np.float64)
    return np.moveaxis((codes * scale).reshape(v.shape), -1, axis)


WIDE = False


def mx_kscale(k):
    if not WIDE:
        return np.ones(k)
    levels = np.array([10, -10, 5, -5, 0])
    if k % 512:
        return np.exp2(np.random.permutation(np.resize(levels, k // 32))).repeat(32)
    a = np.empty((k // 512, 16))
    for p in range(k // 512):
        a[p, :8] = np.random.permutation(np.resize(levels, 8))
        for g in range(8):
            far = levels[np.abs(levels - a[p, g]) >= 10]
            a[p, g + 8] = far[np.random.randint(len(far))]
    return np.exp2(a.ravel()).repeat(32)


def f64(x):
    return np.asarray(x).astype(np.float64)


def striped(idx):
    return np.tile(idx.reshape(-1, 16).T, (8, 1)).astype(np.uint16)


def unstriped(offs):
    return offs[:16].T.reshape(-1).astype(np.int64)


def striped8(idx):
    return np.concatenate([x.reshape(-1, 16).T for x in idx]).astype(np.uint16)


def runs(offs, k):
    lists = np.stack([offs[16 * r : 16 * r + 16].T.reshape(-1) for r in range(8)]).astype(np.int64)
    return lists[np.arange(k) % 512 // 64]


def pack_weight(w):
    k, n = w.shape
    w = f64(np.asarray(w, np.float32).astype(ml_dtypes.bfloat16)).reshape(k // 32, 32, n)
    amax = np.abs(w).max(1)
    byte = np.clip(np.where(amax > 0, np.frexp(amax)[1] - 1 + 127 - 7, 1), 1, 254)
    scaled = (w * np.exp2(127.0 - byte)[:, None, :]).reshape(k, n).astype(np.float32)
    words = np.ascontiguousarray(scaled.reshape(k // 512, 128, 4, n).transpose(0, 1, 3, 2)).astype(ml_dtypes.float8_e4m3fn).view(np.uint8)
    return words, np.ascontiguousarray(byte.astype(np.uint8).reshape(k // 512, 16, n))


def unpack_weight(words, scales):
    g, p, n, _ = words.shape
    vals = np.ascontiguousarray(words).view(ml_dtypes.float8_e4m3fn).astype(np.float64) * np.repeat(np.exp2(scales.astype(np.float64) - 127.0), 8, axis=1)[..., None]
    return vals.transpose(0, 1, 3, 2).reshape(g * 512, n)


E2M1 = np.array([0.0, 0.5, 1.0, 1.5, 2.0, 3.0, 4.0, 6.0, -0.0, -0.5, -1.0, -1.5, -2.0, -3.0, -4.0, -6.0])


def pack_fp4(w):
    k, n = w.shape
    w = f64(np.asarray(w, np.float32).astype(ml_dtypes.bfloat16)).reshape(k // 32, 32, n)
    amax = np.abs(w).max(1)
    mant, ex = np.frexp(amax / 6.0)
    byte = np.clip(np.where(amax > 0, np.where(mant > 0.5, ex, ex - 1) + 127, 1), 1, 254)
    scaled = (w * np.exp2(127.0 - byte)[:, None, :]).reshape(k, n).astype(np.float32)
    c = np.ascontiguousarray(scaled.reshape(k // 512, 128, 4, n).transpose(0, 1, 3, 2)).astype(ml_dtypes.float4_e2m1fn).view(np.uint8) & 0xF
    words = (c[..., 0::2] | (c[..., 1::2] << 4)).reshape(k // 512, 128, 2 * n)
    return np.ascontiguousarray(words), np.ascontiguousarray(byte.astype(np.uint8).reshape(k // 512, 16, n))


def unpack_fp4(words, scales):
    g, _, n = scales.shape
    words = np.ascontiguousarray(words).reshape(g, 128, n, 2)
    nib = np.empty((g, 128, n, 4), np.uint8)
    nib[..., 0::2] = words & 0xF
    nib[..., 1::2] = words >> 4
    vals = E2M1[nib] * np.repeat(np.exp2(scales.astype(np.float64) - 127.0), 8, axis=1)[..., None]
    return vals.transpose(0, 1, 3, 2).reshape(g * 512, n)


def sigmoid(v):
    return 1.0 / (1.0 + np.exp(-np.maximum(v, -700.0)))

def planes(y):
    n, m = y.shape
    v = y.astype(np.float32).astype(ml_dtypes.bfloat16).astype(np.float64).reshape(n // 32, 32, m)
    top = np.abs(v).max(1)
    byte = np.clip(np.where(top > 0, np.frexp(top)[1] - 1 + 127 - 7, 1), 1, 254)
    codes = (v * np.exp2(127.0 - byte)[:, None, :]).reshape(n, m).astype(np.float32).astype(ml_dtypes.float8_e4m3fn).view(np.uint8)
    words = codes.reshape(n // 512, 128, 4, m).transpose(0, 1, 3, 2)
    return np.ascontiguousarray(words), np.ascontiguousarray(byte.astype(np.uint8).reshape(n // 512, 16, m))


K, T, S, V, H = 512, 2048, 512, 512, 512


def setup_inputs():
    n = np.random.standard_normal
    s = mx_kscale(K)[:, None]
    u = mx_kscale(S)
    packed_xT = pack_weight(n((K, T)) * s)
    packed_w1 = pack_fp4(n((K, H)) / np.sqrt(K) / s)
    packed_w2 = pack_fp4(n((K, H)) / np.sqrt(K) / s)
    return {
        "x_words": packed_xT[0],
        "x_scales": packed_xT[1],
        "w1_words": packed_w1[0],
        "w1_scales": packed_w1[1],
        "w2_words": packed_w2[0],
        "w2_scales": packed_w2[1],
        "ga": (np.random.uniform(0.5, 1.5, (H, 1)) * u[:, None]).astype(np.float32),
        "gb": (np.random.uniform(0.5, 1.5, (H, 1)) / u[:, None]).astype(np.float32),
        "offs": striped(np.random.permutation(T)[:S]),
        "two": striped(np.random.permutation(T)[:V]),
        "n1": striped8(np.stack([np.random.permutation(S) for _ in range(8)])),
        "nq": striped8(np.stack([np.random.permutation(V) for _ in range(8)])),
        "cq": striped8(np.stack([np.random.permutation(V) for _ in range(8)])),
    }


def reference(x_words, x_scales, w1_words, w1_scales, w2_words, w2_scales, ga, gb, offs, two, n1, nq, cq):
    xq = unpack_weight(x_words, x_scales)[:, unstriped(offs)]
    a = unpack_fp4(w1_words, w1_scales).T @ xq
    z = f64(ga) * (a / (np.abs(a[np.arange(H)[:, None], runs(n1, H)]) + 0.5))
    x_two = unpack_weight(x_words, x_scales)[:, unstriped(two)]
    b = unpack_fp4(w2_words, w2_scales).T @ x_two
    z2 = f64(gb) * ((b[np.arange(H)[:, None], runs(nq, H)]) / (np.abs(b) + 0.5))
    s = 0.0625 * ((mxq(z, 0, "e4m3").T @ mxq(z2, 0, "e4m3")))
    out_0 = s * (sigmoid(s[np.arange(S)[:, None], runs(cq, S)]))
    return (out_0,) + planes(out_0)

@@ -1,0 +1,239 @@
+from contextlib import ExitStack
+
+import concourse.mybir as mybir
+
+K, T, S, V, H = 512, 2048, 512, 512, 512
+FLOPS = 2 * K * H * S + 2 * K * H * V + 2 * H * S * V
+
+F32 = mybir.dt.float32
+BF16 = mybir.dt.bfloat16
+I32 = mybir.dt.int32
+U32 = mybir.dt.uint32
+U16 = mybir.dt.uint16
+U8 = mybir.dt.uint8
+FP8X4 = mybir.dt.float8_e4m3fn_x4
+FP4X4 = mybir.dt.float4_e2m1fn_x4
+ACT = mybir.ActivationFunctionType
+ALU = mybir.AluOpType
+
+P = 128
+SLOTS = 4
+N = 512
+HALF = N // 2
+LCOLS = N // 16
+CHUNKS = ((0, 256), (256, 128), (384, 128))
+
+
+def tile_picked_keynorm_none_po_kernel(tc, x_words, x_scales, w1_words, w1_scales, w2_words, w2_scales, ga, gb, offs, two, n1, nq, cq, out_0, out_1, out_2):
+    nc = tc.nc
+    with ExitStack() as ctx:
+        sb = ctx.enter_context(tc.tile_pool(name="sb", bufs=1))
+        ps = ctx.enter_context(tc.psum_pool(name="ps", bufs=1))
+
+        def tile(name, shape, dtype):
+            return sb.tile(shape, dtype, name=name, align_bytes=64)
+
+        def bank(index):
+            return ps.tile([P, N], F32, name="bank%d" % index)
+
+        def load_scale_rows(dst, src, queues):
+            for quad, queue in enumerate(queues):
+                queue.dma_start(out=dst[32 * quad : 32 * quad + 4, :].bitcast(I32), in_=src[0, 4 * quad : 4 * quad + 4, :].bitcast(I32))
+
+        def load_list(name, src):
+            dst = tile(name, [P, LCOLS], U16)
+            nc.sync.dma_start(dst[:], src)
+            return dst
+
+        xs = tile("xs", [P, T], U8)
+        nc.vector.memset(xs[:].bitcast(I32), 0)
+        ws_raw = tile("ws_raw", [P, 2 * H], U8)
+        nc.vector.memset(ws_raw[:].bitcast(I32), 0)
+        seed = tile("seed", [P, 8], F32)
+        nc.vector.memset(seed[:], 1.0)
+
+        two_t = load_list("two_t", two)
+        offs_t = load_list("offs_t", offs)
+        nq_t = load_list("nq_t", nq)
+        n1_t = load_list("n1_t", n1)
+        cq_t = load_list("cq_t", cq)
+        w2_raw = tile("w2_raw", [P, 2 * H], U8)
+        nc.scalar.dma_start(out=w2_raw[:].bitcast(I32), in_=w2_words[0].bitcast(I32))
+        w1_raw = tile("w1_raw", [P, 2 * H], U8)
+        nc.scalar.dma_start(out=w1_raw[:].bitcast(I32), in_=w1_words[0].bitcast(I32))
+        xw = tile("xw", [P, T], U32)
+        nc.sync.dma_start(out=xw[:].bitcast(I32), in_=x_words[0].rearrange("p n t -> p (n t)").bitcast(I32))
+        load_scale_rows(xs, x_scales, [nc.scalar] * 4)
+        ga_t = tile("ga_t", [P, SLOTS], F32)
+        nc.gpsimd.dma_start(out=ga_t[:], in_=ga.rearrange("(p t) o -> p (t o)", t=SLOTS))
+        gb_t = tile("gb_t", [P, SLOTS], F32)
+        nc.gpsimd.dma_start(out=gb_t[:], in_=gb.rearrange("(p t) o -> p (t o)", t=SLOTS))
+        load_scale_rows(ws_raw[:, H:], w2_scales, [nc.scalar] * 3 + [nc.gpsimd])
+        preload = tile("preload", [P, 8], F32)
+        nc.scalar.activation(preload[:], seed[:], ACT.Abs_reciprocal_sqrt)
+        load_scale_rows(ws_raw[:, :H], w1_scales, [nc.sync] * 4)
+
+        ga_sign = tile("ga_sign", [P, SLOTS], F32)
+        nc.scalar.activation(ga_sign[:], ga_t[:], ACT.Sign)
+        b_gain = tile("b_gain", [P, SLOTS], F32)
+        nc.vector.tensor_tensor(out=b_gain[:], in0=gb_t[:], in1=ga_sign[:], op=ALU.mult)
+        ga_abs = tile("ga_abs", [P, SLOTS], F32)
+        nc.scalar.activation(ga_abs[:], ga_t[:], ACT.Abs)
+        ga_safe = tile("ga_safe", [P, SLOTS], F32)
+        nc.scalar.activation(ga_safe[:], ga_abs[:], ACT.Copy, bias=1e-30)
+        ga_inv = tile("ga_inv", [P, SLOTS], F32)
+        nc.vector.reciprocal(ga_inv[:], ga_safe[:])
+        ga_inv_half = tile("ga_inv_half", [P, SLOTS], F32)
+        nc.scalar.activation(ga_inv_half[:], ga_inv[:], ACT.Copy, scale=0.5)
+
+        def deal(name, words_raw, scales_raw):
+            words = tile(name + "_words", [P, 2 * H], U8)
+            nc.vector.tensor_copy(
+                out=words[:].rearrange("p (t m b) -> p t m b", t=SLOTS, b=2),
+                in_=words_raw.rearrange("p (m t b) -> p t m b", t=SLOTS, b=2),
+            )
+            scales = tile(name + "_scales", [P, H], U8)
+            nc.vector.tensor_copy(
+                out=scales[:].rearrange("p (t m) -> p t m", t=SLOTS),
+                in_=scales_raw.rearrange("p (m t) -> p t m", t=SLOTS),
+            )
+            return words, scales
+
+        def pick(name, table, dtype, lst):
+            dst = tile(name, [P, N], dtype)
+            nc.vector.tensor_copy(out=dst[:], in_=table[:].indirect(lst[:]))
+            return dst
+
+        def project(first_bank, w_words, w_scales, words, scales):
+            banks = []
+            for t in range(SLOTS):
+                acc = bank(first_bank + t)
+                nc.tensor.matmul_mx(
+                    out=acc[:],
+                    lhsT=w_words[:, 2 * P * t : 2 * P * (t + 1)].bitcast(FP4X4),
+                    lhsT_scale=w_scales[:, P * t : P * (t + 1)],
+                    rhs=words[:].bitcast(FP8X4),
+                    rhs_scale=scales[:],
+                    start=True,
+                    stop=True,
+                )
+                banks.append(acc)
+            return banks
+
+        def half(h):
+            return slice(HALF * h, HALF * (h + 1))
+
+        def list_half(lst, h):
+            return lst[:, LCOLS // 2 * h : LCOLS // 2 * (h + 1)]
+
+        xs_two = pick("xs_two", xs, U8, two_t)
+        xs_idx = pick("xs_idx", xs, U8, offs_t)
+        w2_w, w2_s = deal("w2", w2_raw[:], ws_raw[:, H:])
+        xw_two = pick("xw_two", xw, U32, two_t)
+        b_banks = project(0, w2_w, w2_s, xw_two, xs_two)
+        w1_w, w1_s = deal("w1", w1_raw[:], ws_raw[:, :H])
+        xw_idx = pick("xw_idx", xw, U32, offs_t)
+        a_banks = []
+        for blk in range(SLOTS):
+            acc = bank(4 + blk)
+            for t in range(SLOTS):
+                nc.tensor.matmul_mx(
+                    out=acc[:, P * t : P * (t + 1)],
+                    lhsT=w1_w[:, 2 * P * t : 2 * P * (t + 1)].bitcast(FP4X4),
+                    lhsT_scale=w1_s[:, P * t : P * (t + 1)],
+                    rhs=xw_idx[:, P * blk : P * (blk + 1)].bitcast(FP8X4),
+                    rhs_scale=xs_idx[:, P * blk : P * (blk + 1)],
+                    start=True,
+                    stop=True,
+                )
+            a_banks.append(acc)
+
+        b_near = tile("b_near", [P, SLOTS, N], F32)
+        for t in range(SLOTS):
+            row = tile("b_row%d" % t, [P, N], F32)
+            nc.scalar.activation(row[:], b_banks[t][:], ACT.Copy, scale=b_gain[:, t : t + 1])
+            for h in range(2):
+                nc.vector.tensor_copy(out=b_near[:, t, half(h)], in_=row[:].indirect(list_half(nq_t, h)))
+
+        a_abs = tile("a_abs", [P, SLOTS, N], F32)
+        for blk in range(SLOTS):
+            nc.scalar.activation(a_abs[:, :, P * blk : P * (blk + 1)], a_banks[blk][:].rearrange("p (t c) -> p t c", t=SLOTS), ACT.Abs)
+        a_inv_near = tile("a_inv_near", [P, SLOTS, N], F32)
+        for t in range(SLOTS):
+            win = tile("a_inv%d" % t, [P, 2 * N], F32)
+            nc.scalar.activation(win[:, N:], a_abs[:, t, :], ACT.Abs_reciprocal_sqrt, scale=ga_inv[:, t : t + 1], bias=ga_inv_half[:, t : t + 1])
+            nc.scalar.activation(win[:, :N], win[:, N:], ACT.Square)
+            nc.vector.tensor_copy(out=a_inv_near[:, t, :], in_=win[:].indirect(n1_t[:]))
+        z_bf = tile("z_bf", [P, SLOTS * N], BF16)
+        for blk in range(SLOTS):
+            nc.vector.tensor_tensor(
+                out=z_bf[:].rearrange("p (u m t) -> p m t u", u=SLOTS, t=SLOTS)[:, 32 * blk : 32 * (blk + 1)],
+                in0=a_banks[blk][:].rearrange("p (t m u) -> p m t u", t=SLOTS, u=SLOTS),
+                in1=a_inv_near[:, :, P * blk : P * (blk + 1)].rearrange("p t (m u) -> p m t u", u=SLOTS),
+                op=ALU.mult,
+            )
+        z_words = tile("z_words", [P, N], U32)
+        z_scales = tile("z_scales", [P, N], U8)
+        nc.vector.quantize_mx(out=z_words[:].bitcast(FP8X4), scales=z_scales[:], in_=z_bf[:])
+
+        b_inv = tile("a_abs", [P, SLOTS, N], F32)
+        z2_bf = tile("z2_bf", [P, SLOTS * N], BF16)
+        z2_words = tile("z2_words", [P, N], U32)
+        z2_scales = tile("z2_scales", [P, N], U8)
+        rows = [tile("s_row%d" % u, [P, N], F32) for u in range(SLOTS)]
+        s_banks = {}
+        for h in range(2):
+            for t in range(SLOTS):
+                nc.scalar.activation(b_inv[:, t, half(h)], b_banks[t][:, half(h)], ACT.Abs)
+            nc.scalar.activation(b_inv[:, :, half(h)], b_inv[:, :, half(h)], ACT.Abs_reciprocal_sqrt, bias=0.5)
+            nc.scalar.activation(b_inv[:, :, half(h)], b_inv[:, :, half(h)], ACT.Square)
+            wide = slice(SLOTS * HALF * h, SLOTS * HALF * (h + 1))
+            nc.vector.tensor_tensor(
+                out=z2_bf[:, wide].rearrange("p (c i t) -> p c t i", i=4, t=SLOTS),
+                in0=b_near[:, :, half(h)].rearrange("p t (c i) -> p c t i", i=4),
+                in1=b_inv[:, :, half(h)].rearrange("p t (c i) -> p c t i", i=4),
+                op=ALU.mult,
+            )
+            nc.vector.quantize_mx(out=z2_words[:, half(h)].bitcast(FP8X4), scales=z2_scales[:, half(h)], in_=z2_bf[:, wide])
+            for u in range(SLOTS):
+                acc = bank(4 * (1 - h) + u)
+                nc.tensor.matmul_mx(
+                    out=acc[:, :HALF],
+                    lhsT=z_words[:, P * u : P * (u + 1)].bitcast(FP8X4),
+                    lhsT_scale=z_scales[:, P * u : P * (u + 1)],
+                    rhs=z2_words[:, half(h)].bitcast(FP8X4),
+                    rhs_scale=z2_scales[:, half(h)],
+                    start=True,
+                    stop=True,
+                )
+                s_banks[h, u] = acc
+                nc.scalar.activation(rows[u][:, half(h)], acc[:, :HALF], ACT.Sigmoid if u == 0 else ACT.Copy, scale=0.0625)
+
+        gate = tile("gate", [P, SLOTS, N], F32)
+        res = tile("res", [P, SLOTS, N], F32)
+        res_bf = tile("res_bf", [P, SLOTS * N], BF16)
+        res_words = tile("res_words", [P, N], U32)
+        res_scales = tile("res_scales", [P, N], U8)
+        out_rows = out_0.rearrange("(p u) v -> p u v", u=SLOTS)
+        for first, width in CHUNKS:
+            cols = slice(first, first + width)
+            for u in range(SLOTS):
+                looked_up = rows[u][:].indirect(cq_t[:, first // 16 : (first + width) // 16])
+                if u == 0:
+                    nc.vector.tensor_copy(out=gate[:, u, cols], in_=looked_up)
+                else:
+                    nc.scalar.activation(gate[:, u, cols], looked_up, ACT.Sigmoid)
+                nc.vector.scalar_tensor_tensor(
+                    out=res[:, u, cols], in0=s_banks[first // HALF, u][:, first % HALF : first % HALF + width], scalar=0.0625, in1=gate[:, u, cols], op0=ALU.mult, op1=ALU.mult
+                )
+            nc.sync.dma_start(out=out_rows[:, :, cols], in_=res[:, :, cols])
+            wide = slice(SLOTS * first, SLOTS * (first + width))
+            nc.vector.tensor_copy(
+                out=res_bf[:, wide].rearrange("p (c i u) -> p c u i", i=4, u=SLOTS),
+                in_=res[:, :, cols].rearrange("p u (c i) -> p c u i", i=4),
+            )
+            nc.vector.quantize_mx(out=res_words[:, cols].bitcast(FP8X4), scales=res_scales[:, cols], in_=res_bf[:, wide])
+            nc.sync.dma_start(out=out_1[0].rearrange("p n t -> p (n t)").bitcast(I32)[:, cols], in_=res_words[:, cols].bitcast(I32))
+        for quad in range(4):
+            queue = nc.scalar if quad % 2 else nc.sync
+            queue.dma_start(out=out_2[0, 4 * quad : 4 * quad + 4, :].bitcast(I32), in_=res_scales[32 * quad : 32 * quad + 4, :].bitcast(I32))

@@ -22,6 +22,7 @@ N = 512
 HALF = N // 2
 LCOLS = N // 16
 CHUNKS = ((0, 256), (256, 128), (384, 128))
+EARLY = CHUNKS[-1][0]
 
 
 def tile_picked_keynorm_none_po_kernel(tc, x_words, x_scales, w1_words, w1_scales, w2_words, w2_scales, ga, gb, offs, two, n1, nq, cq, out_0, out_1, out_2):
@@ -46,32 +47,34 @@ def tile_picked_keynorm_none_po_kernel(tc, x_words, x_scales, w1_words, w1_scale
             return dst
 
         xs = tile("xs", [P, T], U8)
-        nc.vector.memset(xs[:].bitcast(I32), 0)
-        ws_raw = tile("ws_raw", [P, 2 * H], U8)
-        nc.vector.memset(ws_raw[:].bitcast(I32), 0)
+        nc.gpsimd.memset(xs[:].bitcast(I32), 0)
+        w2s_raw = tile("w2s_raw", [P, H], U8)
+        nc.gpsimd.memset(w2s_raw[:].bitcast(I32), 0)
+        w1s_raw = tile("w1s_raw", [P, H], U8)
+        nc.gpsimd.memset(w1s_raw[:].bitcast(I32), 0)
         seed = tile("seed", [P, 8], F32)
         nc.vector.memset(seed[:], 1.0)
+        preload = tile("preload", [P, 8], F32)
+        nc.scalar.activation(preload[:], seed[:], ACT.Abs_reciprocal_sqrt)
 
         two_t = load_list("two_t", two)
         offs_t = load_list("offs_t", offs)
-        nq_t = load_list("nq_t", nq)
-        n1_t = load_list("n1_t", n1)
-        cq_t = load_list("cq_t", cq)
         w2_raw = tile("w2_raw", [P, 2 * H], U8)
-        nc.scalar.dma_start(out=w2_raw[:].bitcast(I32), in_=w2_words[0].bitcast(I32))
-        w1_raw = tile("w1_raw", [P, 2 * H], U8)
-        nc.scalar.dma_start(out=w1_raw[:].bitcast(I32), in_=w1_words[0].bitcast(I32))
+        nc.sync.dma_start(out=w2_raw[:].bitcast(I32), in_=w2_words[0].bitcast(I32))
+        load_scale_rows(xs, x_scales, [nc.sync] * 4)
         xw = tile("xw", [P, T], U32)
         nc.sync.dma_start(out=xw[:].bitcast(I32), in_=x_words[0].rearrange("p n t -> p (n t)").bitcast(I32))
-        load_scale_rows(xs, x_scales, [nc.scalar] * 4)
+        load_scale_rows(w2s_raw, w2_scales, [nc.sync] * 4)
+        w1_raw = tile("w1_raw", [P, 2 * H], U8)
+        nc.sync.dma_start(out=w1_raw[:].bitcast(I32), in_=w1_words[0].bitcast(I32))
         ga_t = tile("ga_t", [P, SLOTS], F32)
-        nc.gpsimd.dma_start(out=ga_t[:], in_=ga.rearrange("(p t) o -> p (t o)", t=SLOTS))
+        nc.sync.dma_start(out=ga_t[:], in_=ga.rearrange("(p t) o -> p (t o)", t=SLOTS))
         gb_t = tile("gb_t", [P, SLOTS], F32)
-        nc.gpsimd.dma_start(out=gb_t[:], in_=gb.rearrange("(p t) o -> p (t o)", t=SLOTS))
-        load_scale_rows(ws_raw[:, H:], w2_scales, [nc.scalar] * 3 + [nc.gpsimd])
-        preload = tile("preload", [P, 8], F32)
-        nc.scalar.activation(preload[:], seed[:], ACT.Abs_reciprocal_sqrt)
-        load_scale_rows(ws_raw[:, :H], w1_scales, [nc.sync] * 4)
+        nc.sync.dma_start(out=gb_t[:], in_=gb.rearrange("(p t) o -> p (t o)", t=SLOTS))
+        nq_t = load_list("nq_t", nq)
+        load_scale_rows(w1s_raw, w1_scales, [nc.sync] * 4)
+        n1_t = load_list("n1_t", n1)
+        cq_t = load_list("cq_t", cq)
 
         ga_sign = tile("ga_sign", [P, SLOTS], F32)
         nc.scalar.activation(ga_sign[:], ga_t[:], ACT.Sign)
@@ -86,14 +89,14 @@ def tile_picked_keynorm_none_po_kernel(tc, x_words, x_scales, w1_words, w1_scale
         ga_inv_half = tile("ga_inv_half", [P, SLOTS], F32)
         nc.scalar.activation(ga_inv_half[:], ga_inv[:], ACT.Copy, scale=0.5)
 
-        def deal(name, words_raw, scales_raw):
+        def deal(name, words_raw, scales_raw, engine):
             words = tile(name + "_words", [P, 2 * H], U8)
-            nc.vector.tensor_copy(
+            engine.tensor_copy(
                 out=words[:].rearrange("p (t m b) -> p t m b", t=SLOTS, b=2),
                 in_=words_raw.rearrange("p (m t b) -> p t m b", t=SLOTS, b=2),
             )
             scales = tile(name + "_scales", [P, H], U8)
-            nc.vector.tensor_copy(
+            engine.tensor_copy(
                 out=scales[:].rearrange("p (t m) -> p t m", t=SLOTS),
                 in_=scales_raw.rearrange("p (m t) -> p t m", t=SLOTS),
             )
@@ -128,10 +131,10 @@ def tile_picked_keynorm_none_po_kernel(tc, x_words, x_scales, w1_words, w1_scale
 
         xs_two = pick("xs_two", xs, U8, two_t)
         xs_idx = pick("xs_idx", xs, U8, offs_t)
-        w2_w, w2_s = deal("w2", w2_raw[:], ws_raw[:, H:])
+        w2_w, w2_s = deal("w2", w2_raw[:], w2s_raw[:], nc.gpsimd)
         xw_two = pick("xw_two", xw, U32, two_t)
         b_banks = project(0, w2_w, w2_s, xw_two, xs_two)
-        w1_w, w1_s = deal("w1", w1_raw[:], ws_raw[:, :H])
+        w1_w, w1_s = deal("w1", w1_raw[:], w1s_raw[:], nc.gpsimd)
         xw_idx = pick("xw_idx", xw, U32, offs_t)
         a_banks = []
         for blk in range(SLOTS):
@@ -182,33 +185,38 @@ def tile_picked_keynorm_none_po_kernel(tc, x_words, x_scales, w1_words, w1_scale
         z2_scales = tile("z2_scales", [P, N], U8)
         rows = [tile("s_row%d" % u, [P, N], F32) for u in range(SLOTS)]
         s_banks = {}
-        for h in range(2):
-            for t in range(SLOTS):
-                nc.scalar.activation(b_inv[:, t, half(h)], b_banks[t][:, half(h)], ACT.Abs)
-            nc.scalar.activation(b_inv[:, :, half(h)], b_inv[:, :, half(h)], ACT.Abs_reciprocal_sqrt, bias=0.5)
-            nc.scalar.activation(b_inv[:, :, half(h)], b_inv[:, :, half(h)], ACT.Square)
-            wide = slice(SLOTS * HALF * h, SLOTS * HALF * (h + 1))
+        for t in range(SLOTS):
+            nc.scalar.activation(b_inv[:, t, :], b_banks[t][:], ACT.Abs)
+        early_banks = [bank(4 + u) for u in range(SLOTS)]
+        last_banks = [bank(u) for u in range(SLOTS)]
+        for first, width in CHUNKS:
+            cols = slice(first, first + width)
+            nc.scalar.activation(b_inv[:, :, cols], b_inv[:, :, cols], ACT.Abs_reciprocal_sqrt, bias=0.5)
+            nc.scalar.activation(b_inv[:, :, cols], b_inv[:, :, cols], ACT.Square)
+            wide = slice(SLOTS * first, SLOTS * (first + width))
             nc.vector.tensor_tensor(
                 out=z2_bf[:, wide].rearrange("p (c i t) -> p c t i", i=4, t=SLOTS),
-                in0=b_near[:, :, half(h)].rearrange("p t (c i) -> p c t i", i=4),
-                in1=b_inv[:, :, half(h)].rearrange("p t (c i) -> p c t i", i=4),
+                in0=b_near[:, :, cols].rearrange("p t (c i) -> p c t i", i=4),
+                in1=b_inv[:, :, cols].rearrange("p t (c i) -> p c t i", i=4),
                 op=ALU.mult,
             )
-            nc.vector.quantize_mx(out=z2_words[:, half(h)].bitcast(FP8X4), scales=z2_scales[:, half(h)], in_=z2_bf[:, wide])
+            nc.vector.quantize_mx(out=z2_words[:, cols].bitcast(FP8X4), scales=z2_scales[:, cols], in_=z2_bf[:, wide])
             for u in range(SLOTS):
-                acc = bank(4 * (1 - h) + u)
+                s_banks[first, u] = (early_banks if first < EARLY else last_banks)[u][:, cols]
                 nc.tensor.matmul_mx(
-                    out=acc[:, :HALF],
+                    out=s_banks[first, u],
                     lhsT=z_words[:, P * u : P * (u + 1)].bitcast(FP8X4),
                     lhsT_scale=z_scales[:, P * u : P * (u + 1)],
-                    rhs=z2_words[:, half(h)].bitcast(FP8X4),
-                    rhs_scale=z2_scales[:, half(h)],
+                    rhs=z2_words[:, cols].bitcast(FP8X4),
+                    rhs_scale=z2_scales[:, cols],
                     start=True,
                     stop=True,
                 )
-                s_banks[h, u] = acc
-                nc.scalar.activation(rows[u][:, half(h)], acc[:, :HALF], ACT.Sigmoid if u == 0 else ACT.Copy, scale=0.0625)
-
+        nc.scalar.activation(rows[0][:, :EARLY], early_banks[0][:, :EARLY], ACT.Sigmoid, scale=0.0625)
+        for u in range(SLOTS):
+            if u > 0:
+                nc.vector.tensor_scalar(out=rows[u][:, :EARLY], in0=early_banks[u][:, :EARLY], scalar1=0.0625, scalar2=None, op0=ALU.mult)
+            nc.scalar.activation(rows[u][:, EARLY:], last_banks[u][:, EARLY:], ACT.Sigmoid if u == 0 else ACT.Copy, scale=0.0625)
         gate = tile("gate", [P, SLOTS, N], F32)
         res = tile("res", [P, SLOTS, N], F32)
         res_bf = tile("res_bf", [P, SLOTS * N], BF16)
@@ -224,7 +232,7 @@ def tile_picked_keynorm_none_po_kernel(tc, x_words, x_scales, w1_words, w1_scale
                 else:
                     nc.scalar.activation(gate[:, u, cols], looked_up, ACT.Sigmoid)
                 nc.vector.scalar_tensor_tensor(
-                    out=res[:, u, cols], in0=s_banks[first // HALF, u][:, first % HALF : first % HALF + width], scalar=0.0625, in1=gate[:, u, cols], op0=ALU.mult, op1=ALU.mult
+                    out=res[:, u, cols], in0=s_banks[first, u], scalar=0.0625, in1=gate[:, u, cols], op0=ALU.mult, op1=ALU.mult
                 )
             nc.sync.dma_start(out=out_rows[:, :, cols], in_=res[:, :, cols])
             wide = slice(SLOTS * first, SLOTS * (first + width))

@@ -53,7 +53,7 @@ def tile_picked_keynorm_none_po_kernel(tc, x_words, x_scales, w1_words, w1_scale
         w1s_raw = tile("w1s_raw", [P, H], U8)
         nc.gpsimd.memset(w1s_raw[:].bitcast(I32), 0)
         seed = tile("seed", [P, 8], F32)
-        nc.vector.memset(seed[:], 1.0)
+        nc.vector.memset(seed[:], 0.5)
         preload = tile("preload", [P, 8], F32)
         nc.scalar.activation(preload[:], seed[:], ACT.Abs_reciprocal_sqrt)
 
@@ -79,15 +79,12 @@ def tile_picked_keynorm_none_po_kernel(tc, x_words, x_scales, w1_words, w1_scale
         ga_sign = tile("ga_sign", [P, SLOTS], F32)
         nc.scalar.activation(ga_sign[:], ga_t[:], ACT.Sign)
         b_gain = tile("b_gain", [P, SLOTS], F32)
-        nc.vector.tensor_tensor(out=b_gain[:], in0=gb_t[:], in1=ga_sign[:], op=ALU.mult)
+        for t in range(SLOTS):
+            nc.scalar.activation(b_gain[:, t : t + 1], gb_t[:, t : t + 1], ACT.Copy, scale=ga_sign[:, t : t + 1])
         ga_abs = tile("ga_abs", [P, SLOTS], F32)
         nc.scalar.activation(ga_abs[:], ga_t[:], ACT.Abs)
-        ga_safe = tile("ga_safe", [P, SLOTS], F32)
-        nc.scalar.activation(ga_safe[:], ga_abs[:], ACT.Copy, bias=1e-30)
-        ga_inv = tile("ga_inv", [P, SLOTS], F32)
-        nc.vector.reciprocal(ga_inv[:], ga_safe[:])
-        ga_inv_half = tile("ga_inv_half", [P, SLOTS], F32)
-        nc.scalar.activation(ga_inv_half[:], ga_inv[:], ACT.Copy, scale=0.5)
+        ga_root = tile("ga_root", [P, SLOTS], F32)
+        nc.gpsimd.tensor_tensor(out=ga_root[:], in0=ga_abs[:], in1=seed[:, :SLOTS], op=ALU.pow)
 
         def deal(name, words_raw, scales_raw, engine):
             words = tile(name + "_words", [P, 2 * H], U8)
@@ -136,20 +133,22 @@ def tile_picked_keynorm_none_po_kernel(tc, x_words, x_scales, w1_words, w1_scale
         b_banks = project(0, w2_w, w2_s, xw_two, xs_two)
         w1_w, w1_s = deal("w1", w1_raw[:], w1s_raw[:], nc.gpsimd)
         xw_idx = pick("xw_idx", xw, U32, offs_t)
-        a_banks = []
-        for blk in range(SLOTS):
-            acc = bank(4 + blk)
-            for t in range(SLOTS):
-                nc.tensor.matmul_mx(
-                    out=acc[:, P * t : P * (t + 1)],
-                    lhsT=w1_w[:, 2 * P * t : 2 * P * (t + 1)].bitcast(FP4X4),
-                    lhsT_scale=w1_s[:, P * t : P * (t + 1)],
-                    rhs=xw_idx[:, P * blk : P * (blk + 1)].bitcast(FP8X4),
-                    rhs_scale=xs_idx[:, P * blk : P * (blk + 1)],
-                    start=True,
-                    stop=True,
-                )
-            a_banks.append(acc)
+        a_banks = {}
+        for pair in range(2):
+            for h in range(2):
+                acc = bank(4 + 2 * pair + h)
+                for e in range(2):
+                    t = 2 * pair + e
+                    nc.tensor.matmul_mx(
+                        out=acc[:, half(e)],
+                        lhsT=w1_w[:, 2 * P * t : 2 * P * (t + 1)].bitcast(FP4X4),
+                        lhsT_scale=w1_s[:, P * t : P * (t + 1)],
+                        rhs=xw_idx[:, half(h)].bitcast(FP8X4),
+                        rhs_scale=xs_idx[:, half(h)],
+                        start=True,
+                        stop=True,
+                    )
+                a_banks[pair, h] = acc[:].rearrange("p (e c) -> p e c", e=2)
 
         b_near = tile("b_near", [P, SLOTS, N], F32)
         for t in range(SLOTS):
@@ -159,22 +158,30 @@ def tile_picked_keynorm_none_po_kernel(tc, x_words, x_scales, w1_words, w1_scale
                 nc.vector.tensor_copy(out=b_near[:, t, half(h)], in_=row[:].indirect(list_half(nq_t, h)))
 
         a_abs = tile("a_abs", [P, SLOTS, N], F32)
-        for blk in range(SLOTS):
-            nc.scalar.activation(a_abs[:, :, P * blk : P * (blk + 1)], a_banks[blk][:].rearrange("p (t c) -> p t c", t=SLOTS), ACT.Abs)
         a_inv_near = tile("a_inv_near", [P, SLOTS, N], F32)
-        for t in range(SLOTS):
-            win = tile("a_inv%d" % t, [P, 2 * N], F32)
-            nc.scalar.activation(win[:, N:], a_abs[:, t, :], ACT.Abs_reciprocal_sqrt, scale=ga_inv[:, t : t + 1], bias=ga_inv_half[:, t : t + 1])
-            nc.scalar.activation(win[:, :N], win[:, N:], ACT.Square)
-            nc.vector.tensor_copy(out=a_inv_near[:, t, :], in_=win[:].indirect(n1_t[:]))
+        a_inv = [tile("a_inv%d" % t, [P, 2 * N], F32) for t in range(SLOTS)]
+        for pair in range(2):
+            for h in range(2):
+                nc.scalar.activation(a_abs[:, 2 * pair : 2 * pair + 2, half(h)], a_banks[pair, h], ACT.Abs)
+            for t in (2 * pair, 2 * pair + 1):
+                nc.scalar.activation(a_inv[t][:, N:], a_abs[:, t, :], ACT.Abs_reciprocal_sqrt, bias=0.5)
+            for t in (2 * pair, 2 * pair + 1):
+                nc.scalar.activation(a_inv[t][:, :N], a_inv[t][:, N:], ACT.Square, scale=ga_root[:, t : t + 1])
+                nc.vector.tensor_copy(out=a_inv_near[:, t, :], in_=a_inv[t][:].indirect(n1_t[:]))
+        z_pairs = tile("z_pairs", [P, 2 * 2 * N], BF16)
+        for pair in range(2):
+            for h in range(2):
+                nc.vector.tensor_tensor(
+                    out=z_pairs[:].rearrange("p (r c e) -> p r c e", r=2, e=2)[:, pair, half(h), :],
+                    in0=a_banks[pair, h].rearrange("p e c -> p c e"),
+                    in1=a_inv_near[:, 2 * pair : 2 * pair + 2, half(h)].rearrange("p e c -> p c e"),
+                    op=ALU.mult,
+                )
         z_bf = tile("z_bf", [P, SLOTS * N], BF16)
-        for blk in range(SLOTS):
-            nc.vector.tensor_tensor(
-                out=z_bf[:].rearrange("p (u m t) -> p m t u", u=SLOTS, t=SLOTS)[:, 32 * blk : 32 * (blk + 1)],
-                in0=a_banks[blk][:].rearrange("p (t m u) -> p m t u", t=SLOTS, u=SLOTS),
-                in1=a_inv_near[:, :, P * blk : P * (blk + 1)].rearrange("p t (m u) -> p m t u", u=SLOTS),
-                op=ALU.mult,
-            )
+        nc.vector.tensor_copy(
+            out=z_bf[:].bitcast(F32).rearrange("p (u m r) -> p m u r", u=SLOTS, r=2),
+            in_=z_pairs[:].bitcast(F32).rearrange("p (r m u) -> p m u r", r=2, u=SLOTS),
+        )
         z_words = tile("z_words", [P, N], U32)
         z_scales = tile("z_scales", [P, N], U8)
         nc.vector.quantize_mx(out=z_words[:].bitcast(FP8X4), scales=z_scales[:], in_=z_bf[:])
@@ -189,9 +196,15 @@ def tile_picked_keynorm_none_po_kernel(tc, x_words, x_scales, w1_words, w1_scale
             nc.scalar.activation(b_inv[:, t, :], b_banks[t][:], ACT.Abs)
         early_banks = [bank(4 + u) for u in range(SLOTS)]
         last_banks = [bank(u) for u in range(SLOTS)]
-        for first, width in CHUNKS:
-            cols = slice(first, first + width)
+        def b_root(chunk):
+            cols = slice(chunk[0], chunk[0] + chunk[1])
             nc.scalar.activation(b_inv[:, :, cols], b_inv[:, :, cols], ACT.Abs_reciprocal_sqrt, bias=0.5)
+
+        b_root(CHUNKS[0])
+        for index, (first, width) in enumerate(CHUNKS):
+            cols = slice(first, first + width)
+            if index + 1 < len(CHUNKS):
+                b_root(CHUNKS[index + 1])
             nc.scalar.activation(b_inv[:, :, cols], b_inv[:, :, cols], ACT.Square)
             wide = slice(SLOTS * first, SLOTS * (first + width))
             nc.vector.tensor_tensor(

from contextlib import ExitStack

import concourse.mybir as mybir

K, T, S, V, H = 512, 2048, 512, 512, 512
FLOPS = 2 * K * H * S + 2 * K * H * V + 2 * H * S * V

F32 = mybir.dt.float32
BF16 = mybir.dt.bfloat16
I32 = mybir.dt.int32
U32 = mybir.dt.uint32
U16 = mybir.dt.uint16
U8 = mybir.dt.uint8
FP8X4 = mybir.dt.float8_e4m3fn_x4
FP4X4 = mybir.dt.float4_e2m1fn_x4
ACT = mybir.ActivationFunctionType
ALU = mybir.AluOpType

P = 128
SLOTS = 4
N = 512
HALF = N // 2
LCOLS = N // 16
CHUNKS = ((0, 256), (256, 128), (384, 128))
EARLY = CHUNKS[-1][0]


def tile_picked_keynorm_none_po_kernel(tc, x_words, x_scales, w1_words, w1_scales, w2_words, w2_scales, ga, gb, offs, two, n1, nq, cq, out_0, out_1, out_2):
    nc = tc.nc
    with ExitStack() as ctx:
        sb = ctx.enter_context(tc.tile_pool(name="sb", bufs=1))
        ps = ctx.enter_context(tc.psum_pool(name="ps", bufs=1))

        def tile(name, shape, dtype):
            return sb.tile(shape, dtype, name=name, align_bytes=64)

        def bank(index):
            return ps.tile([P, N], F32, name="bank%d" % index)

        def load_scale_rows(dst, src, queues):
            for quad, queue in enumerate(queues):
                queue.dma_start(out=dst[32 * quad : 32 * quad + 4, :].bitcast(I32), in_=src[0, 4 * quad : 4 * quad + 4, :].bitcast(I32))

        def load_list(name, src):
            dst = tile(name, [P, LCOLS], U16)
            nc.sync.dma_start(dst[:], src)
            return dst

        xs = tile("xs", [P, T], U8)
        nc.gpsimd.memset(xs[:].bitcast(I32), 0)
        w2s_raw = tile("w2s_raw", [P, H], U8)
        nc.gpsimd.memset(w2s_raw[:].bitcast(I32), 0)
        w1s_raw = tile("w1s_raw", [P, H], U8)
        nc.gpsimd.memset(w1s_raw[:].bitcast(I32), 0)
        seed = tile("seed", [P, 8], F32)
        nc.vector.memset(seed[:], 0.5)
        preload = tile("preload", [P, 8], F32)
        nc.scalar.activation(preload[:], seed[:], ACT.Abs_reciprocal_sqrt)

        two_t = load_list("two_t", two)
        offs_t = load_list("offs_t", offs)
        w2_raw = tile("w2_raw", [P, 2 * H], U8)
        nc.sync.dma_start(out=w2_raw[:].bitcast(I32), in_=w2_words[0].bitcast(I32))
        load_scale_rows(xs, x_scales, [nc.sync] * 4)
        xw = tile("xw", [P, T], U32)
        nc.sync.dma_start(out=xw[:].bitcast(I32), in_=x_words[0].rearrange("p n t -> p (n t)").bitcast(I32))
        load_scale_rows(w2s_raw, w2_scales, [nc.sync] * 4)
        w1_raw = tile("w1_raw", [P, 2 * H], U8)
        nc.sync.dma_start(out=w1_raw[:].bitcast(I32), in_=w1_words[0].bitcast(I32))
        ga_t = tile("ga_t", [P, SLOTS], F32)
        nc.sync.dma_start(out=ga_t[:], in_=ga.rearrange("(p t) o -> p (t o)", t=SLOTS))
        gb_t = tile("gb_t", [P, SLOTS], F32)
        nc.sync.dma_start(out=gb_t[:], in_=gb.rearrange("(p t) o -> p (t o)", t=SLOTS))
        nq_t = load_list("nq_t", nq)
        load_scale_rows(w1s_raw, w1_scales, [nc.sync] * 4)
        n1_t = load_list("n1_t", n1)
        cq_t = load_list("cq_t", cq)

        ga_sign = tile("ga_sign", [P, SLOTS], F32)
        nc.scalar.activation(ga_sign[:], ga_t[:], ACT.Sign)
        b_gain = tile("b_gain", [P, SLOTS], F32)
        for t in range(SLOTS):
            nc.scalar.activation(b_gain[:, t : t + 1], gb_t[:, t : t + 1], ACT.Copy, scale=ga_sign[:, t : t + 1])
        ga_abs = tile("ga_abs", [P, SLOTS], F32)
        nc.scalar.activation(ga_abs[:], ga_t[:], ACT.Abs)
        ga_root = tile("ga_root", [P, SLOTS], F32)
        nc.gpsimd.tensor_tensor(out=ga_root[:], in0=ga_abs[:], in1=seed[:, :SLOTS], op=ALU.pow)

        def deal(name, words_raw, scales_raw, engine):
            words = tile(name + "_words", [P, 2 * H], U8)
            engine.tensor_copy(
                out=words[:].rearrange("p (t m b) -> p t m b", t=SLOTS, b=2),
                in_=words_raw.rearrange("p (m t b) -> p t m b", t=SLOTS, b=2),
            )
            scales = tile(name + "_scales", [P, H], U8)
            engine.tensor_copy(
                out=scales[:].rearrange("p (t m) -> p t m", t=SLOTS),
                in_=scales_raw.rearrange("p (m t) -> p t m", t=SLOTS),
            )
            return words, scales

        def pick(name, table, dtype, lst):
            dst = tile(name, [P, N], dtype)
            nc.vector.tensor_copy(out=dst[:], in_=table[:].indirect(lst[:]))
            return dst

        def project(first_bank, w_words, w_scales, words, scales):
            banks = []
            for t in range(SLOTS):
                acc = bank(first_bank + t)
                nc.tensor.matmul_mx(
                    out=acc[:],
                    lhsT=w_words[:, 2 * P * t : 2 * P * (t + 1)].bitcast(FP4X4),
                    lhsT_scale=w_scales[:, P * t : P * (t + 1)],
                    rhs=words[:].bitcast(FP8X4),
                    rhs_scale=scales[:],
                    start=True,
                    stop=True,
                )
                banks.append(acc)
            return banks

        def half(h):
            return slice(HALF * h, HALF * (h + 1))

        def list_half(lst, h):
            return lst[:, LCOLS // 2 * h : LCOLS // 2 * (h + 1)]

        xs_two = pick("xs_two", xs, U8, two_t)
        xs_idx = pick("xs_idx", xs, U8, offs_t)
        w2_w, w2_s = deal("w2", w2_raw[:], w2s_raw[:], nc.gpsimd)
        xw_two = pick("xw_two", xw, U32, two_t)
        b_banks = project(0, w2_w, w2_s, xw_two, xs_two)
        w1_w, w1_s = deal("w1", w1_raw[:], w1s_raw[:], nc.gpsimd)
        xw_idx = pick("xw_idx", xw, U32, offs_t)
        a_banks = {}
        for pair in range(2):
            for h in range(2):
                acc = bank(4 + 2 * pair + h)
                for e in range(2):
                    t = 2 * pair + e
                    nc.tensor.matmul_mx(
                        out=acc[:, half(e)],
                        lhsT=w1_w[:, 2 * P * t : 2 * P * (t + 1)].bitcast(FP4X4),
                        lhsT_scale=w1_s[:, P * t : P * (t + 1)],
                        rhs=xw_idx[:, half(h)].bitcast(FP8X4),
                        rhs_scale=xs_idx[:, half(h)],
                        start=True,
                        stop=True,
                    )
                a_banks[pair, h] = acc[:].rearrange("p (e c) -> p e c", e=2)

        b_near = tile("b_near", [P, SLOTS, N], F32)
        for t in range(SLOTS):
            row = tile("b_row%d" % t, [P, N], F32)
            nc.scalar.activation(row[:], b_banks[t][:], ACT.Copy, scale=b_gain[:, t : t + 1])
            for h in range(2):
                nc.vector.tensor_copy(out=b_near[:, t, half(h)], in_=row[:].indirect(list_half(nq_t, h)))

        a_abs = tile("a_abs", [P, SLOTS, N], F32)
        a_inv_near = tile("a_inv_near", [P, SLOTS, N], F32)
        a_inv = [tile("a_inv%d" % t, [P, 2 * N], F32) for t in range(SLOTS)]
        for pair in range(2):
            for h in range(2):
                nc.scalar.activation(a_abs[:, 2 * pair : 2 * pair + 2, half(h)], a_banks[pair, h], ACT.Abs)
            for t in (2 * pair, 2 * pair + 1):
                nc.scalar.activation(a_inv[t][:, N:], a_abs[:, t, :], ACT.Abs_reciprocal_sqrt, bias=0.5)
            for t in (2 * pair, 2 * pair + 1):
                nc.scalar.activation(a_inv[t][:, :N], a_inv[t][:, N:], ACT.Square, scale=ga_root[:, t : t + 1])
                nc.vector.tensor_copy(out=a_inv_near[:, t, :], in_=a_inv[t][:].indirect(n1_t[:]))
        z_pairs = tile("z_pairs", [P, 2 * 2 * N], BF16)
        for pair in range(2):
            for h in range(2):
                nc.vector.tensor_tensor(
                    out=z_pairs[:].rearrange("p (r c e) -> p r c e", r=2, e=2)[:, pair, half(h), :],
                    in0=a_banks[pair, h].rearrange("p e c -> p c e"),
                    in1=a_inv_near[:, 2 * pair : 2 * pair + 2, half(h)].rearrange("p e c -> p c e"),
                    op=ALU.mult,
                )
        z_bf = tile("z_bf", [P, SLOTS * N], BF16)
        nc.vector.tensor_copy(
            out=z_bf[:].bitcast(F32).rearrange("p (u m r) -> p m u r", u=SLOTS, r=2),
            in_=z_pairs[:].bitcast(F32).rearrange("p (r m u) -> p m u r", r=2, u=SLOTS),
        )
        z_words = tile("z_words", [P, N], U32)
        z_scales = tile("z_scales", [P, N], U8)
        nc.vector.quantize_mx(out=z_words[:].bitcast(FP8X4), scales=z_scales[:], in_=z_bf[:])

        b_inv = tile("a_abs", [P, SLOTS, N], F32)
        z2_bf = tile("z2_bf", [P, SLOTS * N], BF16)
        z2_words = tile("z2_words", [P, N], U32)
        z2_scales = tile("z2_scales", [P, N], U8)
        rows = [tile("s_row%d" % u, [P, N], F32) for u in range(SLOTS)]
        s_banks = {}
        for t in range(SLOTS):
            nc.scalar.activation(b_inv[:, t, :], b_banks[t][:], ACT.Abs)
        early_banks = [bank(4 + u) for u in range(SLOTS)]
        last_banks = [bank(u) for u in range(SLOTS)]
        def b_root(chunk):
            cols = slice(chunk[0], chunk[0] + chunk[1])
            nc.scalar.activation(b_inv[:, :, cols], b_inv[:, :, cols], ACT.Abs_reciprocal_sqrt, bias=0.5)

        b_root(CHUNKS[0])
        for index, (first, width) in enumerate(CHUNKS):
            cols = slice(first, first + width)
            if index + 1 < len(CHUNKS):
                b_root(CHUNKS[index + 1])
            nc.scalar.activation(b_inv[:, :, cols], b_inv[:, :, cols], ACT.Square)
            wide = slice(SLOTS * first, SLOTS * (first + width))
            nc.vector.tensor_tensor(
                out=z2_bf[:, wide].rearrange("p (c i t) -> p c t i", i=4, t=SLOTS),
                in0=b_near[:, :, cols].rearrange("p t (c i) -> p c t i", i=4),
                in1=b_inv[:, :, cols].rearrange("p t (c i) -> p c t i", i=4),
                op=ALU.mult,
            )
            nc.vector.quantize_mx(out=z2_words[:, cols].bitcast(FP8X4), scales=z2_scales[:, cols], in_=z2_bf[:, wide])
            for u in range(SLOTS):
                s_banks[first, u] = (early_banks if first < EARLY else last_banks)[u][:, cols]
                nc.tensor.matmul_mx(
                    out=s_banks[first, u],
                    lhsT=z_words[:, P * u : P * (u + 1)].bitcast(FP8X4),
                    lhsT_scale=z_scales[:, P * u : P * (u + 1)],
                    rhs=z2_words[:, cols].bitcast(FP8X4),
                    rhs_scale=z2_scales[:, cols],
                    start=True,
                    stop=True,
                )
        nc.scalar.activation(rows[0][:, :EARLY], early_banks[0][:, :EARLY], ACT.Sigmoid, scale=0.0625)
        for u in range(SLOTS):
            if u > 0:
                nc.vector.tensor_scalar(out=rows[u][:, :EARLY], in0=early_banks[u][:, :EARLY], scalar1=0.0625, scalar2=None, op0=ALU.mult)
            nc.scalar.activation(rows[u][:, EARLY:], last_banks[u][:, EARLY:], ACT.Sigmoid if u == 0 else ACT.Copy, scale=0.0625)
        gate = tile("gate", [P, SLOTS, N], F32)
        res = tile("res", [P, SLOTS, N], F32)
        res_bf = tile("res_bf", [P, SLOTS * N], BF16)
        res_words = tile("res_words", [P, N], U32)
        res_scales = tile("res_scales", [P, N], U8)
        out_rows = out_0.rearrange("(p u) v -> p u v", u=SLOTS)
        for first, width in CHUNKS:
            cols = slice(first, first + width)
            for u in range(SLOTS):
                looked_up = rows[u][:].indirect(cq_t[:, first // 16 : (first + width) // 16])
                if u == 0:
                    nc.vector.tensor_copy(out=gate[:, u, cols], in_=looked_up)
                else:
                    nc.scalar.activation(gate[:, u, cols], looked_up, ACT.Sigmoid)
                nc.vector.scalar_tensor_tensor(
                    out=res[:, u, cols], in0=s_banks[first, u], scalar=0.0625, in1=gate[:, u, cols], op0=ALU.mult, op1=ALU.mult
                )
            nc.sync.dma_start(out=out_rows[:, :, cols], in_=res[:, :, cols])
            wide = slice(SLOTS * first, SLOTS * (first + width))
            nc.vector.tensor_copy(
                out=res_bf[:, wide].rearrange("p (c i u) -> p c u i", i=4, u=SLOTS),
                in_=res[:, :, cols].rearrange("p u (c i) -> p c u i", i=4),
            )
            nc.vector.quantize_mx(out=res_words[:, cols].bitcast(FP8X4), scales=res_scales[:, cols], in_=res_bf[:, wide])
            nc.sync.dma_start(out=out_1[0].rearrange("p n t -> p (n t)").bitcast(I32)[:, cols], in_=res_words[:, cols].bitcast(I32))
        for quad in range(4):
            queue = nc.scalar if quad % 2 else nc.sync
            queue.dma_start(out=out_2[0, 4 * quad : 4 * quad + 4, :].bitcast(I32), in_=res_scales[32 * quad : 32 * quad + 4, :].bitcast(I32))
